import numpy as np
import ml_dtypes


def mxq(x, axis, fmt="e4m3"):
    dtype, down = {"e4m3": (ml_dtypes.float8_e4m3fn, 7), "e5m2": (ml_dtypes.float8_e5m2, 14)}[fmt]
    v = np.moveaxis(np.asarray(x, np.float32).astype(ml_dtypes.bfloat16).astype(np.float64), axis, -1)
    blocks = v.reshape(v.shape[:-1] + (-1, 32))
    amax = np.abs(blocks).max(-1, keepdims=True)
    byte = np.maximum(np.where(amax > 0, np.frexp(amax)[1] - 1 + 127, 0) - down, 1)
    scale = np.exp2(byte - 127.0)
    codes = (blocks / scale).astype(np.float32).astype(dtype).astype(np.float64)
    return np.moveaxis((codes * scale).reshape(v.shape), -1, axis)


WIDE = False


def mx_kscale(k):
    if not WIDE:
        return np.ones(k)
    levels = np.array([10, -10, 5, -5, 0])
    if k % 512:
        return np.exp2(np.random.permutation(np.resize(levels, k // 32))).repeat(32)
    a = np.empty((k // 512, 16))
    for p in range(k // 512):
        a[p, :8] = np.random.permutation(np.resize(levels, 8))
        for g in range(8):
            far = levels[np.abs(levels - a[p, g]) >= 10]
            a[p, g + 8] = far[np.random.randint(len(far))]
    return np.exp2(a.ravel()).repeat(32)


def f64(x):
    return np.asarray(x).astype(np.float64)


def striped(idx):
    return np.tile(idx.reshape(-1, 16).T, (8, 1)).astype(np.uint16)


def unstriped(offs):
    return offs[:16].T.reshape(-1).astype(np.int64)


def striped8(idx):
    return np.concatenate([x.reshape(-1, 16).T for x in idx]).astype(np.uint16)


def runs(offs, k):
    lists = np.stack([offs[16 * r : 16 * r + 16].T.reshape(-1) for r in range(8)]).astype(np.int64)
    return lists[np.arange(k) % 512 // 64]


def pack_weight(w):
    k, n = w.shape
    w = f64(np.asarray(w, np.float32).astype(ml_dtypes.bfloat16)).reshape(k // 32, 32, n)
    amax = np.abs(w).max(1)
    byte = np.clip(np.where(amax > 0, np.frexp(amax)[1] - 1 + 127 - 7, 1), 1, 254)
    scaled = (w * np.exp2(127.0 - byte)[:, None, :]).reshape(k, n).astype(np.float32)
    words = np.ascontiguousarray(scaled.reshape(k // 512, 128, 4, n).transpose(0, 1, 3, 2)).astype(ml_dtypes.float8_e4m3fn).view(np.uint8)
    return words, np.ascontiguousarray(byte.astype(np.uint8).reshape(k // 512, 16, n))


def unpack_weight(words, scales):
    g, p, n, _ = words.shape
    vals = np.ascontiguousarray(words).view(ml_dtypes.float8_e4m3fn).astype(np.float64) * np.repeat(np.exp2(scales.astype(np.float64) - 127.0), 8, axis=1)[..., None]
    return vals.transpose(0, 1, 3, 2).reshape(g * 512, n)


K, T, S, H, W, G, U = 512, 1024, 256, 512, 128, 2048, 512


def setup_inputs():
    n = np.random.standard_normal
    s = mx_kscale(K)[:, None]
    packed_xT = pack_weight(n((K, T)) * s)
    packed_w1 = pack_weight(n((K, H)) / np.sqrt(2 * K) / s)
    packed_w2 = pack_weight(n((K, H)) / np.sqrt(2 * K) / s)
    packed_dT = pack_weight(n((K, G)) / s)
    perm = np.random.permutation(S)
    perm2 = np.random.permutation(S)
    perm3 = np.random.permutation(U)
    return {
        "x_words": packed_xT[0],
        "x_scales": packed_xT[1],
        "w1_words": packed_w1[0],
        "w1_scales": packed_w1[1],
        "w2_words": packed_w2[0],
        "w2_scales": packed_w2[1],
        "gs": (np.random.uniform(0.5, 1.5, (K, 1)) * s).astype(np.float32),
        "d_words": packed_dT[0],
        "d_scales": packed_dT[1],
        "offs": striped(np.random.permutation(T)[:S]),
        "two": striped(np.random.permutation(T)[:S]),
        "n1": striped(perm[:W]),
        "n2": striped(perm[W:]),
        "n3": striped(perm2[:W]),
        "n4": striped(perm2[W:]),
        "n5": striped(np.random.permutation(S)),
        "ka": striped8(np.random.randint(0, G, (8, H))),
        "kb": striped8(np.random.randint(0, G, (8, H))),
        "n6": striped(perm3[:S]),
        "n7": striped(perm3[S:]),
        "n8": striped(np.random.permutation(S)),
    }


def reference(x_words, x_scales, w1_words, w1_scales, w2_words, w2_scales, gs, d_words, d_scales, offs, two, n1, n2, n3, n4, n5, ka, kb, n6, n7, n8):
    d_ka = unpack_weight(d_words, d_scales)[np.arange(K)[:, None], runs(ka, K)]
    xq = unpack_weight(x_words, x_scales)[:, unstriped(offs)]
    x_two = unpack_weight(x_words, x_scales)[:, unstriped(two)]
    y = unpack_weight(w1_words, w1_scales).T @ xq + unpack_weight(w2_words, w2_scales).T @ x_two
    pa = y[:, unstriped(n1)]
    pb = y[:, unstriped(n2)]
    rb = np.maximum(pa, pb)
    ra = pa + pb
    ua = np.zeros((H, S))
    ua[:, unstriped(n3)] = ra
    ub = ua.copy()
    ub[:, unstriped(n4)] = rb
    z = f64(gs) * (ub - ub[:, unstriped(n5)])
    zq = mxq(z, 0, "e4m3")
    d_kb = unpack_weight(d_words, d_scales)[np.arange(K)[:, None], runs(kb, K)]
    h2 = 0.0625 * (d_ka.T @ zq + d_kb.T @ zq)
    dn = np.minimum(h2, h2[:, unstriped(n8)])
    up = np.maximum(h2, h2[:, unstriped(n8)])
    ph = np.zeros((H, U))
    ph[:, unstriped(n6)] = up
    out = ph.copy()
    out[:, unstriped(n7)] = dn
    return out

@@ -1,0 +1,183 @@
+from contextlib import ExitStack
+
+import concourse.mybir as mybir
+
+K, T, S, H, W, G, U = 512, 1024, 256, 512, 128, 2048, 512
+FLOPS = 2 * (2 * K * H * S) + 2 * (2 * K * H * S)
+
+F32 = mybir.dt.float32
+BF16 = mybir.dt.bfloat16
+I32 = mybir.dt.int32
+U32 = mybir.dt.uint32
+U16 = mybir.dt.uint16
+U8 = mybir.dt.uint8
+FP8X4 = mybir.dt.float8_e4m3fn_x4
+ALU = mybir.AluOpType
+COPY = mybir.ActivationFunctionType.Copy
+
+P = 128
+PACK = 4
+QUAD = 32
+HALF = S // 2
+
+
+def words_of(packed):
+    return packed[0].rearrange("p n r -> p (n r)").bitcast(I32)
+
+
+def tile_picked_dttzacphdpagmx_none_p_kernel(tc, x_words, x_scales, w1_words, w1_scales, w2_words, w2_scales, gs, d_words, d_scales, offs, two, n1, n2, n3, n4, n5, ka, kb, n6, n7, n8, out):
+    nc = tc.nc
+    with ExitStack() as ctx:
+        sb = ctx.enter_context(tc.tile_pool(name="sb", bufs=1))
+        ps = ctx.enter_context(tc.psum_pool(name="ps", bufs=1))
+
+        def load_list(name, src):
+            tile = sb.tile(list(src.shape), U16, name=name)
+            nc.sync.dma_start(tile[:], src)
+            return tile
+
+        xw = sb.tile([P, T], U32, name="xw", align_bytes=64)
+        xs = sb.tile([P, T], U8, name="xs", align_bytes=64)
+        ws = sb.tile([P, H], U8, name="ws", align_bytes=64)
+        nc.gpsimd.memset(xs[:].bitcast(I32), 0)
+        nc.gpsimd.memset(ws[:].bitcast(I32), 0)
+
+        l_offs = load_list("l_offs", offs)
+        l_two = load_list("l_two", two)
+        nc.sync.dma_start(xw[:].bitcast(I32), words_of(x_words))
+        for q in range(4):
+            nc.sync.dma_start(xs[QUAD * q : QUAD * q + 4, :].bitcast(I32), x_scales[0, 4 * q : 4 * q + 4, :].bitcast(I32))
+        w_raw = [sb.tile([P, H], U32, name=f"w_raw{a}", align_bytes=64) for a in range(2)]
+        nc.sync.dma_start(w_raw[0][:].bitcast(I32), words_of(w1_words))
+        nc.sync.dma_start(w_raw[1][:].bitcast(I32), words_of(w2_words))
+        for q in range(4):
+            nc.sync.dma_start(ws[QUAD * q : QUAD * q + 4, :].bitcast(I32), w1_scales[0, 4 * q : 4 * q + 4, :].bitcast(I32))
+        for q in range(4):
+            eng = nc.gpsimd if q >= 2 else nc.sync
+            eng.dma_start(ws[QUAD * q + 4 : QUAD * q + 8, :].bitcast(I32), w2_scales[0, 4 * q : 4 * q + 4, :].bitcast(I32))
+        l_n1 = load_list("l_n1", n1)
+        l_n2 = load_list("l_n2", n2)
+        l_n3 = load_list("l_n3", n3)
+        l_n4 = load_list("l_n4", n4)
+        l_ka = load_list("l_ka", ka)
+        l_kb = load_list("l_kb", kb)
+        ds = sb.tile([P, G], U8, name="ds", tag="ds", align_bytes=64)
+        nc.vector.memset(ds[:].bitcast(I32), 0)
+        seat = (0, 1, 16, 17)
+        for r in range(4):
+            nc.sync.dma_start(ds[seat[r] : P : QUAD, :].bitcast(I32), d_scales[0, r:16:4, :].bitcast(I32))
+        dw = sb.tile([P, G], U32, name="dw", tag="dw", align_bytes=64)
+        nc.sync.dma_start(dw[:].bitcast(I32), words_of(d_words))
+        gain = sb.tile([P, PACK], F32, name="gain")
+        nc.sync.dma_start(gain[:], gs.rearrange("(p t) o -> p (t o)", t=PACK))
+        l_n5 = load_list("l_n5", n5)
+        l_n8 = load_list("l_n8", n8)
+        l_n6 = load_list("l_n6", n6)
+        l_n7 = load_list("l_n7", n7)
+
+        pages = [sb.tile([P, U], F32, name=f"page{i}") for i in range(4)]
+        nc.vector.memset(pages[0][:], 0.0)
+        for i in range(1, 4):
+            nc.scalar.activation(pages[i][:], pages[0][:], COPY)
+        ub = [sb.tile([P, S], F32, name=f"ub{t}", tag=f"ub{t}") for t in range(PACK)]
+        for t in range(PACK):
+            nc.vector.memset(ub[t][:], 0.0)
+        dsc = sb.tile([P, 2 * H], U8, name="dsc", align_bytes=64)
+        nc.vector.memset(dsc[:].bitcast(I32), 0)
+
+        xgw = [sb.tile([P, S], U32, name=f"xgw{a}", align_bytes=64) for a in range(2)]
+        xgs = [sb.tile([P, S], U8, name=f"xgs{a}", align_bytes=64) for a in range(2)]
+        for a, lst in enumerate((l_offs, l_two)):
+            nc.vector.tensor_copy(xgw[a][:], xw[:].indirect(lst[:]))
+            nc.vector.tensor_copy(xgs[a][:], xs[:].indirect(lst[:]))
+
+        wd = [sb.tile([P, H], U32, name=f"wd{a}", align_bytes=64) for a in range(2)]
+        wsd = sb.tile([P, H], U8, name="wsd", align_bytes=64)
+        y = [sb.tile([P, S], F32, name=f"y{t}", tag=("y0", "first", "y2", "y3")[t]) for t in range(PACK)]
+        pab = sb.tile([P, PACK, S], F32, name="pab")
+        for t in range(PACK):
+            cols = slice(P * t, P * (t + 1))
+            for a in range(2):
+                nc.scalar.copy(wd[a][:, cols], w_raw[a][:, t:H:PACK])
+            nc.vector.tensor_copy(wsd[:, cols], ws[:, t:H:PACK])
+        for t in range(PACK):
+            cols = slice(P * t, P * (t + 1))
+            acc = ps.tile([P, S], F32, name=f"acc_y{t}")
+            for a in range(2):
+                nc.tensor.matmul_mx(acc[:], lhsT=wd[a][:, cols].bitcast(FP8X4), lhsT_scale=wsd[4 * a : P, cols],
+                                    rhs=xgw[a][:].bitcast(FP8X4), rhs_scale=xgs[a][:], start=(a == 0), stop=(a == 1))
+            nc.vector.tensor_copy(y[t][:], acc[:])
+            nc.scalar.activation(pab[:, t, 0:W], y[t][:].indirect(l_n1[:]), COPY)
+            nc.scalar.activation(pab[:, t, W:S], y[t][:].indirect(l_n2[:]), COPY)
+        ra = sb.tile([P, PACK, W], F32, name="ra", tag="first")
+        rb = sb.tile([P, PACK, W], F32, name="rb")
+        for t in range(PACK):
+            nc.vector.tensor_tensor(ra[:, t, :], pab[:, t, 0:W], pab[:, t, W:S], ALU.add)
+            nc.vector.tensor_tensor(rb[:, t, :], pab[:, t, 0:W], pab[:, t, W:S], ALU.max)
+            nc.scalar.activation(ub[t][:].indirect(l_n3[:]), ra[:, t, :], COPY)
+            nc.scalar.activation(ub[t][:].indirect(l_n4[:]), rb[:, t, :], COPY)
+
+        dgs = sb.tile([P, 2 * H], U8, name="dgs", align_bytes=64)
+        for a, lst in enumerate((l_ka, l_kb)):
+            for c in range(2):
+                nc.vector.tensor_copy(dgs[:, H * a + 256 * c : H * a + 256 * (c + 1)], ds[:].indirect(lst[:, 16 * c : 16 * (c + 1)]))
+        for r in range(4):
+            nc.sync.dma_start(dsc[r:P:QUAD, :].bitcast(I32), dgs[seat[r] : P : QUAD, :].bitcast(I32))
+        dgw = [sb.tile([P, H], U32, name=f"dgw{a}", tag=("ds", "dgw1")[a], align_bytes=64) for a in range(2)]
+        for a, lst in enumerate((l_ka, l_kb)):
+            for c in range(2):
+                nc.vector.tensor_copy(dgw[a][:, 256 * c : 256 * (c + 1)], dw[:].indirect(lst[:, 16 * c : 16 * (c + 1)]))
+
+        ug = sb.tile([P, PACK, S], F32, name="ug", tag="dw", align_bytes=64)
+        for t in range(PACK):
+            nc.vector.tensor_scalar(ug[:, t, :], ub[t][:], gain[:, t : t + 1], None, ALU.mult)
+
+        h = sb.tile([P, 4, S], F32, name="h")
+        zw, zs = [], []
+        for c, tag in enumerate(("first", "ub3")):
+            g5 = sb.tile([P, PACK, HALF], F32, name=f"g5_{c}", tag=tag)
+            zb = sb.tile([P, HALF * PACK], BF16, name=f"zb{c}", tag="zb", align_bytes=64)
+            zw.append(sb.tile([P, HALF], U32, name=f"zw{c}", align_bytes=64))
+            zs.append(sb.tile([P, HALF], U8, name=f"zs{c}", align_bytes=64))
+            for t in range(PACK):
+                nc.scalar.activation(g5[:, t, :], ug[:, t, :].indirect(l_n5[:, 8 * c : 8 * (c + 1)]), COPY)
+            nc.vector.tensor_tensor(
+                zb[:].rearrange("p (c i t) -> p c t i", i=4, t=PACK),
+                ug[:, :, HALF * c : HALF * (c + 1)].rearrange("p t (c i) -> p c t i", i=4),
+                g5[:].rearrange("p t (c i) -> p c t i", i=4),
+                ALU.subtract,
+            )
+            nc.vector.quantize_mx(out=zw[c][:].bitcast(FP8X4), scales=zs[c][:], in_=zb[:])
+
+        def second(acc, i, c):
+            for a in range(2):
+                nc.tensor.matmul_mx(acc, lhsT=dgw[a][:, P * i : P * (i + 1)].bitcast(FP8X4),
+                                    lhsT_scale=dsc[:, H * a + P * i : H * a + P * (i + 1)],
+                                    rhs=zw[c][:].bitcast(FP8X4), rhs_scale=zs[c][:], start=(a == 0), stop=(a == 1))
+
+        for c in range(2):
+            acc_first = ps.tile([P, HALF], F32, name=f"acc_first{c}")
+            second(acc_first[:], 0, c)
+            nc.scalar.activation(h[:, 0, HALF * c : HALF * (c + 1)], acc_first[:], COPY, scale=0.0625)
+        for c in range(2):
+            acc_rest = ps.tile([P, 3, HALF], F32, name=f"acc_rest{c}")
+            for i in range(1, 4):
+                second(acc_rest[:, i - 1, :], i, c)
+            nc.vector.tensor_scalar(h[:, 1:4, HALF * c : HALF * (c + 1)], acc_rest[:], 0.0625, None, ALU.mult)
+
+        g8 = sb.tile([P, 4, S], F32, name="g8")
+        up = sb.tile([P, 4, S], F32, name="up")
+        dn = sb.tile([P, 4, S], F32, name="dn")
+        for i in range(4):
+            for c in range(2):
+                nc.scalar.activation(g8[:, i, HALF * c : HALF * (c + 1)], h[:, i, :].indirect(l_n8[:, 8 * c : 8 * (c + 1)]), COPY)
+        for i in range(4):
+            nc.vector.tensor_tensor(up[:, i, :], h[:, i, :], g8[:, i, :], ALU.max)
+            nc.vector.tensor_tensor(dn[:, i, :], h[:, i, :], g8[:, i, :], ALU.min)
+            nc.scalar.activation(pages[i][:].indirect(l_n6[:]), up[:, i, :], COPY)
+            nc.scalar.activation(pages[i][:].indirect(l_n7[:]), dn[:, i, :], COPY)
+            if i < 3:
+                nc.sync.dma_start(out[P * i : P * (i + 1), :], pages[i][:])
+            else:
+                nc.scalar.dma_start(out[P * i : P * (i + 1), 0:S], pages[i][:, 0:S])
+                nc.sync.dma_start(out[P * i : P * (i + 1), S:U], pages[i][:, S:U])

@@ -39,8 +39,8 @@ def tile_picked_dttzacphdpagmx_none_p_kernel(tc, x_words, x_scales, w1_words, w1
         xw = sb.tile([P, T], U32, name="xw", align_bytes=64)
         xs = sb.tile([P, T], U8, name="xs", align_bytes=64)
         ws = sb.tile([P, H], U8, name="ws", align_bytes=64)
-        nc.gpsimd.memset(xs[:].bitcast(I32), 0)
-        nc.gpsimd.memset(ws[:].bitcast(I32), 0)
+        nc.vector.memset(xs[:].bitcast(I32), 0)
+        nc.vector.memset(ws[:].bitcast(I32), 0)
 
         l_offs = load_list("l_offs", offs)
         l_two = load_list("l_two", two)
@@ -48,13 +48,20 @@ def tile_picked_dttzacphdpagmx_none_p_kernel(tc, x_words, x_scales, w1_words, w1
         for q in range(4):
             nc.sync.dma_start(xs[QUAD * q : QUAD * q + 4, :].bitcast(I32), x_scales[0, 4 * q : 4 * q + 4, :].bitcast(I32))
         w_raw = [sb.tile([P, H], U32, name=f"w_raw{a}", align_bytes=64) for a in range(2)]
+
+        def load_w_scales(a, q):
+            src = (w1_scales, w2_scales)[a]
+            first = QUAD * q + 4 * a
+            nc.sync.dma_start(ws[first : first + 4, :].bitcast(I32), src[0, 4 * q : 4 * q + 4, :].bitcast(I32))
+
         nc.sync.dma_start(w_raw[0][:].bitcast(I32), words_of(w1_words))
+        for q in range(2):
+            load_w_scales(0, q)
         nc.sync.dma_start(w_raw[1][:].bitcast(I32), words_of(w2_words))
+        for q in range(2, 4):
+            load_w_scales(0, q)
         for q in range(4):
-            nc.sync.dma_start(ws[QUAD * q : QUAD * q + 4, :].bitcast(I32), w1_scales[0, 4 * q : 4 * q + 4, :].bitcast(I32))
-        for q in range(4):
-            eng = nc.gpsimd if q >= 2 else nc.sync
-            eng.dma_start(ws[QUAD * q + 4 : QUAD * q + 8, :].bitcast(I32), w2_scales[0, 4 * q : 4 * q + 4, :].bitcast(I32))
+            load_w_scales(1, q)
         l_n1 = load_list("l_n1", n1)
         l_n2 = load_list("l_n2", n2)
         l_n3 = load_list("l_n3", n3)
@@ -102,7 +109,7 @@ def tile_picked_dttzacphdpagmx_none_p_kernel(tc, x_words, x_scales, w1_words, w1
             nc.vector.tensor_copy(wsd[:, cols], ws[:, t:H:PACK])
         for t in range(PACK):
             cols = slice(P * t, P * (t + 1))
-            acc = ps.tile([P, S], F32, name=f"acc_y{t}")
+            acc = ps.tile([P, S], F32, name=f"acc_y{t}", tag=f"bank{t}")
             for a in range(2):
                 nc.tensor.matmul_mx(acc[:], lhsT=wd[a][:, cols].bitcast(FP8X4), lhsT_scale=wsd[4 * a : P, cols],
                                     rhs=xgw[a][:].bitcast(FP8X4), rhs_scale=xgs[a][:], start=(a == 0), stop=(a == 1))
@@ -132,7 +139,9 @@ def tile_picked_dttzacphdpagmx_none_p_kernel(tc, x_words, x_scales, w1_words, w1
         for t in range(PACK):
             nc.vector.tensor_scalar(ug[:, t, :], ub[t][:], gain[:, t : t + 1], None, ALU.mult)
 
-        h = sb.tile([P, 4, S], F32, name="h")
+        h = [sb.tile([P, S + 16], F32, name=f"h{i}") for i in range(4)]
+        for i in range(4):
+            nc.vector.memset(h[i][:, S : S + 16], 0.0)
         zw, zs = [], []
         for c, tag in enumerate(("first", "ub3")):
             g5 = sb.tile([P, PACK, HALF], F32, name=f"g5_{c}", tag=tag)
@@ -156,28 +165,23 @@ def tile_picked_dttzacphdpagmx_none_p_kernel(tc, x_words, x_scales, w1_words, w1
                                     rhs=zw[c][:].bitcast(FP8X4), rhs_scale=zs[c][:], start=(a == 0), stop=(a == 1))
 
         for c in range(2):
-            acc_first = ps.tile([P, HALF], F32, name=f"acc_first{c}")
-            second(acc_first[:], 0, c)
-            nc.scalar.activation(h[:, 0, HALF * c : HALF * (c + 1)], acc_first[:], COPY, scale=0.0625)
-        for c in range(2):
-            acc_rest = ps.tile([P, 3, HALF], F32, name=f"acc_rest{c}")
-            for i in range(1, 4):
-                second(acc_rest[:, i - 1, :], i, c)
-            nc.vector.tensor_scalar(h[:, 1:4, HALF * c : HALF * (c + 1)], acc_rest[:], 0.0625, None, ALU.mult)
+            cols = slice(HALF * c, HALF * (c + 1))
+            for i in range(4):
+                acc = ps.tile([P, HALF], F32, name=f"acc_h{c}{i}", tag=f"bank{4 * c + i}")
+                second(acc[:], i, c)
+                if c == 0 or i == 0:
+                    nc.scalar.activation(h[i][:, cols], acc[:], COPY, scale=0.0625)
+                else:
+                    nc.vector.tensor_scalar(h[i][:, cols], acc[:], 0.0625, None, ALU.mult)
 
         g8 = sb.tile([P, 4, S], F32, name="g8")
         up = sb.tile([P, 4, S], F32, name="up")
         dn = sb.tile([P, 4, S], F32, name="dn")
         for i in range(4):
-            for c in range(2):
-                nc.scalar.activation(g8[:, i, HALF * c : HALF * (c + 1)], h[:, i, :].indirect(l_n8[:, 8 * c : 8 * (c + 1)]), COPY)
+            nc.scalar.activation(g8[:, i, :], h[i][:].indirect(l_n8[:]), COPY)
         for i in range(4):
-            nc.vector.tensor_tensor(up[:, i, :], h[:, i, :], g8[:, i, :], ALU.max)
-            nc.vector.tensor_tensor(dn[:, i, :], h[:, i, :], g8[:, i, :], ALU.min)
+            nc.vector.tensor_tensor(up[:, i, :], h[i][:, 0:S], g8[:, i, :], ALU.max)
+            nc.vector.tensor_tensor(dn[:, i, :], h[i][:, 0:S], g8[:, i, :], ALU.min)
             nc.scalar.activation(pages[i][:].indirect(l_n6[:]), up[:, i, :], COPY)
             nc.scalar.activation(pages[i][:].indirect(l_n7[:]), dn[:, i, :], COPY)
-            if i < 3:
-                nc.sync.dma_start(out[P * i : P * (i + 1), :], pages[i][:])
-            else:
-                nc.scalar.dma_start(out[P * i : P * (i + 1), 0:S], pages[i][:, 0:S])
-                nc.sync.dma_start(out[P * i : P * (i + 1), S:U], pages[i][:, S:U])
+            nc.sync.dma_start(out[P * i : P * (i + 1), :], pages[i][:])

@@ -64,10 +64,6 @@ def tile_picked_dttzacphdpagmx_none_p_kernel(tc, x_words, x_scales, w1_words, w1
             load_w_scales(1, q)
         l_n1 = load_list("l_n1", n1)
         l_n2 = load_list("l_n2", n2)
-        l_n3 = load_list("l_n3", n3)
-        l_n4 = load_list("l_n4", n4)
-        l_ka = load_list("l_ka", ka)
-        l_kb = load_list("l_kb", kb)
         ds = sb.tile([P, G], U8, name="ds", tag="ds", align_bytes=64)
         nc.vector.memset(ds[:].bitcast(I32), 0)
         seat = (0, 1, 16, 17)
@@ -75,6 +71,10 @@ def tile_picked_dttzacphdpagmx_none_p_kernel(tc, x_words, x_scales, w1_words, w1
             nc.sync.dma_start(ds[seat[r] : P : QUAD, :].bitcast(I32), d_scales[0, r:16:4, :].bitcast(I32))
         dw = sb.tile([P, G], U32, name="dw", tag="dw", align_bytes=64)
         nc.sync.dma_start(dw[:].bitcast(I32), words_of(d_words))
+        l_n3 = load_list("l_n3", n3)
+        l_n4 = load_list("l_n4", n4)
+        l_ka = load_list("l_ka", ka)
+        l_kb = load_list("l_kb", kb)
         gain = sb.tile([P, PACK], F32, name="gain")
         nc.sync.dma_start(gain[:], gs.rearrange("(p t) o -> p (t o)", t=PACK))
         l_n5 = load_list("l_n5", n5)
@@ -86,7 +86,7 @@ def tile_picked_dttzacphdpagmx_none_p_kernel(tc, x_words, x_scales, w1_words, w1
         nc.vector.memset(pages[0][:], 0.0)
         for i in range(1, 4):
             nc.scalar.activation(pages[i][:], pages[0][:], COPY)
-        ub = [sb.tile([P, S], F32, name=f"ub{t}", tag=f"ub{t}") for t in range(PACK)]
+        ub = [sb.tile([P, S], F32, name=f"ub{t}", tag=f"ub{t}", align_bytes=64) for t in range(PACK)]
         for t in range(PACK):
             nc.vector.memset(ub[t][:], 0.0)
         dsc = sb.tile([P, 2 * H], U8, name="dsc", align_bytes=64)
@@ -100,7 +100,7 @@ def tile_picked_dttzacphdpagmx_none_p_kernel(tc, x_words, x_scales, w1_words, w1
 
         wd = [sb.tile([P, H], U32, name=f"wd{a}", align_bytes=64) for a in range(2)]
         wsd = sb.tile([P, H], U8, name="wsd", align_bytes=64)
-        y = [sb.tile([P, S], F32, name=f"y{t}", tag=("y0", "first", "y2", "y3")[t]) for t in range(PACK)]
+        y = [sb.tile([P, S], F32, name=f"y{t}", tag=("y0", "first", "y2", "y3")[t], align_bytes=64) for t in range(PACK)]
         pab = sb.tile([P, PACK, S], F32, name="pab")
         for t in range(PACK):
             cols = slice(P * t, P * (t + 1))
@@ -116,7 +116,7 @@ def tile_picked_dttzacphdpagmx_none_p_kernel(tc, x_words, x_scales, w1_words, w1
             nc.vector.tensor_copy(y[t][:], acc[:])
             nc.scalar.activation(pab[:, t, 0:W], y[t][:].indirect(l_n1[:]), COPY)
             nc.scalar.activation(pab[:, t, W:S], y[t][:].indirect(l_n2[:]), COPY)
-        ra = sb.tile([P, PACK, W], F32, name="ra", tag="first")
+        ra = sb.tile([P, PACK, W], F32, name="ra", tag="first", align_bytes=64)
         rb = sb.tile([P, PACK, W], F32, name="rb")
         for t in range(PACK):
             nc.vector.tensor_tensor(ra[:, t, :], pab[:, t, 0:W], pab[:, t, W:S], ALU.add)
@@ -124,7 +124,7 @@ def tile_picked_dttzacphdpagmx_none_p_kernel(tc, x_words, x_scales, w1_words, w1
             nc.scalar.activation(ub[t][:].indirect(l_n3[:]), ra[:, t, :], COPY)
             nc.scalar.activation(ub[t][:].indirect(l_n4[:]), rb[:, t, :], COPY)
 
-        dgs = sb.tile([P, 2 * H], U8, name="dgs", align_bytes=64)
+        dgs = sb.tile([P, 2 * H], U8, name="dgs", tag="y0", align_bytes=64)
         for a, lst in enumerate((l_ka, l_kb)):
             for c in range(2):
                 nc.vector.tensor_copy(dgs[:, H * a + 256 * c : H * a + 256 * (c + 1)], ds[:].indirect(lst[:, 16 * c : 16 * (c + 1)]))
@@ -144,7 +144,7 @@ def tile_picked_dttzacphdpagmx_none_p_kernel(tc, x_words, x_scales, w1_words, w1
             nc.vector.memset(h[i][:, S : S + 16], 0.0)
         zw, zs = [], []
         for c, tag in enumerate(("first", "ub3")):
-            g5 = sb.tile([P, PACK, HALF], F32, name=f"g5_{c}", tag=tag)
+            g5 = sb.tile([P, PACK, HALF], F32, name=f"g5_{c}", tag=tag, align_bytes=64)
             zb = sb.tile([P, HALF * PACK], BF16, name=f"zb{c}", tag="zb", align_bytes=64)
             zw.append(sb.tile([P, HALF], U32, name=f"zw{c}", align_bytes=64))
             zs.append(sb.tile([P, HALF], U8, name=f"zs{c}", align_bytes=64))

@@ -100,7 +100,7 @@ def tile_picked_dttzacphdpagmx_none_p_kernel(tc, x_words, x_scales, w1_words, w1
 
         wd = [sb.tile([P, H], U32, name=f"wd{a}", align_bytes=64) for a in range(2)]
         wsd = sb.tile([P, H], U8, name="wsd", align_bytes=64)
-        y = [sb.tile([P, S], F32, name=f"y{t}", tag=("y0", "first", "y2", "y3")[t], align_bytes=64) for t in range(PACK)]
+        y = [sb.tile([P, S], F32, name=f"y{t}", tag=("y0", "y1", "first", "y3")[t], align_bytes=64) for t in range(PACK)]
         pab = sb.tile([P, PACK, S], F32, name="pab")
         for t in range(PACK):
             cols = slice(P * t, P * (t + 1))

from contextlib import ExitStack

import concourse.mybir as mybir

K, T, S, H, W, G, U = 512, 1024, 256, 512, 128, 2048, 512
FLOPS = 2 * (2 * K * H * S) + 2 * (2 * K * H * S)

F32 = mybir.dt.float32
BF16 = mybir.dt.bfloat16
I32 = mybir.dt.int32
U32 = mybir.dt.uint32
U16 = mybir.dt.uint16
U8 = mybir.dt.uint8
FP8X4 = mybir.dt.float8_e4m3fn_x4
ALU = mybir.AluOpType
COPY = mybir.ActivationFunctionType.Copy

P = 128
PACK = 4
QUAD = 32
HALF = S // 2


def words_of(packed):
    return packed[0].rearrange("p n r -> p (n r)").bitcast(I32)


def tile_picked_dttzacphdpagmx_none_p_kernel(tc, x_words, x_scales, w1_words, w1_scales, w2_words, w2_scales, gs, d_words, d_scales, offs, two, n1, n2, n3, n4, n5, ka, kb, n6, n7, n8, out):
    nc = tc.nc
    with ExitStack() as ctx:
        sb = ctx.enter_context(tc.tile_pool(name="sb", bufs=1))
        ps = ctx.enter_context(tc.psum_pool(name="ps", bufs=1))

        def load_list(name, src):
            tile = sb.tile(list(src.shape), U16, name=name)
            nc.sync.dma_start(tile[:], src)
            return tile

        xw = sb.tile([P, T], U32, name="xw", align_bytes=64)
        xs = sb.tile([P, T], U8, name="xs", align_bytes=64)
        ws = sb.tile([P, H], U8, name="ws", align_bytes=64)
        nc.vector.memset(xs[:].bitcast(I32), 0)
        nc.vector.memset(ws[:].bitcast(I32), 0)

        l_offs = load_list("l_offs", offs)
        l_two = load_list("l_two", two)
        nc.sync.dma_start(xw[:].bitcast(I32), words_of(x_words))
        for q in range(4):
            nc.sync.dma_start(xs[QUAD * q : QUAD * q + 4, :].bitcast(I32), x_scales[0, 4 * q : 4 * q + 4, :].bitcast(I32))
        w_raw = [sb.tile([P, H], U32, name=f"w_raw{a}", align_bytes=64) for a in range(2)]

        def load_w_scales(a, q):
            src = (w1_scales, w2_scales)[a]
            first = QUAD * q + 4 * a
            nc.sync.dma_start(ws[first : first + 4, :].bitcast(I32), src[0, 4 * q : 4 * q + 4, :].bitcast(I32))

        nc.sync.dma_start(w_raw[0][:].bitcast(I32), words_of(w1_words))
        for q in range(2):
            load_w_scales(0, q)
        nc.sync.dma_start(w_raw[1][:].bitcast(I32), words_of(w2_words))
        for q in range(2, 4):
            load_w_scales(0, q)
        for q in range(4):
            load_w_scales(1, q)
        l_n1 = load_list("l_n1", n1)
        l_n2 = load_list("l_n2", n2)
        ds = sb.tile([P, G], U8, name="ds", tag="ds", align_bytes=64)
        nc.vector.memset(ds[:].bitcast(I32), 0)
        seat = (0, 1, 16, 17)
        for r in range(4):
            nc.sync.dma_start(ds[seat[r] : P : QUAD, :].bitcast(I32), d_scales[0, r:16:4, :].bitcast(I32))
        dw = sb.tile([P, G], U32, name="dw", tag="dw", align_bytes=64)
        nc.sync.dma_start(dw[:].bitcast(I32), words_of(d_words))
        l_n3 = load_list("l_n3", n3)
        l_n4 = load_list("l_n4", n4)
        l_ka = load_list("l_ka", ka)
        l_kb = load_list("l_kb", kb)
        gain = sb.tile([P, PACK], F32, name="gain")
        nc.sync.dma_start(gain[:], gs.rearrange("(p t) o -> p (t o)", t=PACK))
        l_n5 = load_list("l_n5", n5)
        l_n8 = load_list("l_n8", n8)
        l_n6 = load_list("l_n6", n6)
        l_n7 = load_list("l_n7", n7)

        pages = [sb.tile([P, U], F32, name=f"page{i}") for i in range(4)]
        nc.vector.memset(pages[0][:], 0.0)
        for i in range(1, 4):
            nc.scalar.activation(pages[i][:], pages[0][:], COPY)
        ub = [sb.tile([P, S], F32, name=f"ub{t}", tag=f"ub{t}", align_bytes=64) for t in range(PACK)]
        for t in range(PACK):
            nc.vector.memset(ub[t][:], 0.0)
        dsc = sb.tile([P, 2 * H], U8, name="dsc", align_bytes=64)
        nc.vector.memset(dsc[:].bitcast(I32), 0)

        xgw = [sb.tile([P, S], U32, name=f"xgw{a}", align_bytes=64) for a in range(2)]
        xgs = [sb.tile([P, S], U8, name=f"xgs{a}", align_bytes=64) for a in range(2)]
        for a, lst in enumerate((l_offs, l_two)):
            nc.vector.tensor_copy(xgw[a][:], xw[:].indirect(lst[:]))
            nc.vector.tensor_copy(xgs[a][:], xs[:].indirect(lst[:]))

        wd = [sb.tile([P, H], U32, name=f"wd{a}", align_bytes=64) for a in range(2)]
        wsd = sb.tile([P, H], U8, name="wsd", align_bytes=64)
        y = [sb.tile([P, S], F32, name=f"y{t}", tag=("y0", "y1", "first", "y3")[t], align_bytes=64) for t in range(PACK)]
        pab = sb.tile([P, PACK, S], F32, name="pab")
        for t in range(PACK):
            cols = slice(P * t, P * (t + 1))
            for a in range(2):
                nc.scalar.copy(wd[a][:, cols], w_raw[a][:, t:H:PACK])
            nc.vector.tensor_copy(wsd[:, cols], ws[:, t:H:PACK])
        for t in range(PACK):
            cols = slice(P * t, P * (t + 1))
            acc = ps.tile([P, S], F32, name=f"acc_y{t}", tag=f"bank{t}")
            for a in range(2):
                nc.tensor.matmul_mx(acc[:], lhsT=wd[a][:, cols].bitcast(FP8X4), lhsT_scale=wsd[4 * a : P, cols],
                                    rhs=xgw[a][:].bitcast(FP8X4), rhs_scale=xgs[a][:], start=(a == 0), stop=(a == 1))
            nc.vector.tensor_copy(y[t][:], acc[:])
            nc.scalar.activation(pab[:, t, 0:W], y[t][:].indirect(l_n1[:]), COPY)
            nc.scalar.activation(pab[:, t, W:S], y[t][:].indirect(l_n2[:]), COPY)
        ra = sb.tile([P, PACK, W], F32, name="ra", tag="first", align_bytes=64)
        rb = sb.tile([P, PACK, W], F32, name="rb")
        for t in range(PACK):
            nc.vector.tensor_tensor(ra[:, t, :], pab[:, t, 0:W], pab[:, t, W:S], ALU.add)
            nc.vector.tensor_tensor(rb[:, t, :], pab[:, t, 0:W], pab[:, t, W:S], ALU.max)
            nc.scalar.activation(ub[t][:].indirect(l_n3[:]), ra[:, t, :], COPY)
            nc.scalar.activation(ub[t][:].indirect(l_n4[:]), rb[:, t, :], COPY)

        dgs = sb.tile([P, 2 * H], U8, name="dgs", tag="y0", align_bytes=64)
        for a, lst in enumerate((l_ka, l_kb)):
            for c in range(2):
                nc.vector.tensor_copy(dgs[:, H * a + 256 * c : H * a + 256 * (c + 1)], ds[:].indirect(lst[:, 16 * c : 16 * (c + 1)]))
        for r in range(4):
            nc.sync.dma_start(dsc[r:P:QUAD, :].bitcast(I32), dgs[seat[r] : P : QUAD, :].bitcast(I32))
        dgw = [sb.tile([P, H], U32, name=f"dgw{a}", tag=("ds", "dgw1")[a], align_bytes=64) for a in range(2)]
        for a, lst in enumerate((l_ka, l_kb)):
            for c in range(2):
                nc.vector.tensor_copy(dgw[a][:, 256 * c : 256 * (c + 1)], dw[:].indirect(lst[:, 16 * c : 16 * (c + 1)]))

        ug = sb.tile([P, PACK, S], F32, name="ug", tag="dw", align_bytes=64)
        for t in range(PACK):
            nc.vector.tensor_scalar(ug[:, t, :], ub[t][:], gain[:, t : t + 1], None, ALU.mult)

        h = [sb.tile([P, S + 16], F32, name=f"h{i}") for i in range(4)]
        for i in range(4):
            nc.vector.memset(h[i][:, S : S + 16], 0.0)
        zw, zs = [], []
        for c, tag in enumerate(("first", "ub3")):
            g5 = sb.tile([P, PACK, HALF], F32, name=f"g5_{c}", tag=tag, align_bytes=64)
            zb = sb.tile([P, HALF * PACK], BF16, name=f"zb{c}", tag="zb", align_bytes=64)
            zw.append(sb.tile([P, HALF], U32, name=f"zw{c}", align_bytes=64))
            zs.append(sb.tile([P, HALF], U8, name=f"zs{c}", align_bytes=64))
            for t in range(PACK):
                nc.scalar.activation(g5[:, t, :], ug[:, t, :].indirect(l_n5[:, 8 * c : 8 * (c + 1)]), COPY)
            nc.vector.tensor_tensor(
                zb[:].rearrange("p (c i t) -> p c t i", i=4, t=PACK),
                ug[:, :, HALF * c : HALF * (c + 1)].rearrange("p t (c i) -> p c t i", i=4),
                g5[:].rearrange("p t (c i) -> p c t i", i=4),
                ALU.subtract,
            )
            nc.vector.quantize_mx(out=zw[c][:].bitcast(FP8X4), scales=zs[c][:], in_=zb[:])

        def second(acc, i, c):
            for a in range(2):
                nc.tensor.matmul_mx(acc, lhsT=dgw[a][:, P * i : P * (i + 1)].bitcast(FP8X4),
                                    lhsT_scale=dsc[:, H * a + P * i : H * a + P * (i + 1)],
                                    rhs=zw[c][:].bitcast(FP8X4), rhs_scale=zs[c][:], start=(a == 0), stop=(a == 1))

        for c in range(2):
            cols = slice(HALF * c, HALF * (c + 1))
            for i in range(4):
                acc = ps.tile([P, HALF], F32, name=f"acc_h{c}{i}", tag=f"bank{4 * c + i}")
                second(acc[:], i, c)
                if c == 0 or i == 0:
                    nc.scalar.activation(h[i][:, cols], acc[:], COPY, scale=0.0625)
                else:
                    nc.vector.tensor_scalar(h[i][:, cols], acc[:], 0.0625, None, ALU.mult)

        g8 = sb.tile([P, 4, S], F32, name="g8")
        up = sb.tile([P, 4, S], F32, name="up")
        dn = sb.tile([P, 4, S], F32, name="dn")
        for i in range(4):
            nc.scalar.activation(g8[:, i, :], h[i][:].indirect(l_n8[:]), COPY)
        for i in range(4):
            nc.vector.tensor_tensor(up[:, i, :], h[i][:, 0:S], g8[:, i, :], ALU.max)
            nc.vector.tensor_tensor(dn[:, i, :], h[i][:, 0:S], g8[:, i, :], ALU.min)
            nc.scalar.activation(pages[i][:].indirect(l_n6[:]), up[:, i, :], COPY)
            nc.scalar.activation(pages[i][:].indirect(l_n7[:]), dn[:, i, :], COPY)
            nc.sync.dma_start(out[P * i : P * (i + 1), :], pages[i][:])
